import numpy as np
import ml_dtypes


def mxq(x, axis, fmt="e4m3"):
    dtype, down = {"e4m3": (ml_dtypes.float8_e4m3fn, 7), "e5m2": (ml_dtypes.float8_e5m2, 14)}[fmt]
    v = np.moveaxis(np.asarray(x, np.float32).astype(ml_dtypes.bfloat16).astype(np.float64), axis, -1)
    blocks = v.reshape(v.shape[:-1] + (-1, 32))
    amax = np.abs(blocks).max(-1, keepdims=True)
    byte = np.maximum(np.where(amax > 0, np.frexp(amax)[1] - 1 + 127, 0) - down, 1)
    scale = np.exp2(byte - 127.0)
    codes = (blocks / scale).astype(np.float32).astype(dtype).astype(np.float64)
    return np.moveaxis((codes * scale).reshape(v.shape), -1, axis)


WIDE = False


def mx_kscale(k):
    if not WIDE:
        return np.ones(k)
    levels = np.array([10, -10, 5, -5, 0])
    if k % 512:
        return np.exp2(np.random.permutation(np.resize(levels, k // 32))).repeat(32)
    a = np.empty((k // 512, 16))
    for p in range(k // 512):
        a[p, :8] = np.random.permutation(np.resize(levels, 8))
        for g in range(8):
            far = levels[np.abs(levels - a[p, g]) >= 10]
            a[p, g + 8] = far[np.random.randint(len(far))]
    return np.exp2(a.ravel()).repeat(32)


def f64(x):
    return np.asarray(x).astype(np.float64)


def striped(idx):
    return np.tile(idx.reshape(-1, 16).T, (8, 1)).astype(np.uint16)


def unstriped(offs):
    return offs[:16].T.reshape(-1).astype(np.int64)


E2M1 = np.array([0.0, 0.5, 1.0, 1.5, 2.0, 3.0, 4.0, 6.0, -0.0, -0.5, -1.0, -1.5, -2.0, -3.0, -4.0, -6.0])


def pack_weight(w, fmt):
    k, n = w.shape
    w = f64(np.asarray(w, np.float32).astype(ml_dtypes.bfloat16)).reshape(k // 32, 32, n)
    amax = np.abs(w).max(1)
    if fmt == "e4m3":
        byte = np.frexp(amax)[1] - 1 + 127 - 7
    else:
        mant, ex = np.frexp(amax / 6.0)
        byte = np.where(mant > 0.5, ex, ex - 1) + 127
    byte = np.clip(np.where(amax > 0, byte, 1), 1, 254)
    scaled = (w * np.exp2(127.0 - byte)[:, None, :]).reshape(k, n).astype(np.float32)
    by_word = np.ascontiguousarray(scaled.reshape(k // 512, 128, 4, n).transpose(0, 1, 3, 2))
    if fmt == "e4m3":
        words = by_word.astype(ml_dtypes.float8_e4m3fn).view(np.uint8)
    else:
        c = by_word.astype(ml_dtypes.float4_e2m1fn).view(np.uint8) & 0xF
        words = (c[..., 0::2] | (c[..., 1::2] << 4)).reshape(k // 512, 128, 2 * n)
    return np.ascontiguousarray(words), np.ascontiguousarray(byte.astype(np.uint8).reshape(k // 512, 16, n))


def unpack_weight(words, scales, fmt):
    g, _, n = scales.shape
    words = np.ascontiguousarray(words).reshape(g, 128, n, -1)
    if fmt == "e4m3":
        vals = words.view(ml_dtypes.float8_e4m3fn).astype(np.float64)
    else:
        nib = np.empty((g, 128, n, 4), np.uint8)
        nib[..., 0::2] = words & 0xF
        nib[..., 1::2] = words >> 4
        vals = E2M1[nib]
    vals = vals * np.repeat(np.exp2(scales.astype(np.float64) - 127.0), 8, axis=1)[..., None]
    return vals.transpose(0, 1, 3, 2).reshape(g * 512, n)


K, T, E, C, N = 2048, 512, 2, 256, 256


def by_expert(wq, xq):
    return np.concatenate([wq[e].T @ xq[:, e * C:(e + 1) * C] for e in range(E)], axis=1)


def setup_inputs():
    n = np.random.standard_normal
    s = mx_kscale(K)[:, None]
    w = [pack_weight(m, "e2m1") for m in n((E, K, N)) / np.sqrt(K) / s[None]]
    return {
        "xT": (n((K, T)) * s).astype(np.float32),
        "w_words": np.stack([m[0] for m in w]),
        "w_scales": np.stack([m[1] for m in w]),
        "gate": np.tile(np.random.uniform(0.2, 1.0, E * C), (N, 1)).astype(np.float32),
        "offs": striped(np.random.permutation(T)[:E * C]),
        "dst": striped(np.random.permutation(T)[:E * C]),
    }


def reference(xT, w_words, w_scales, gate, offs, dst):
    idx = unstriped(offs)
    w = np.stack([unpack_weight(w_words[e], w_scales[e], "e2m1") for e in range(E)])
    xq = mxq(f64(xT)[:, idx], 0, "e4m3")
    y = by_expert(w, xq)
    out = np.zeros((N, T))
    out[:, unstriped(dst)] = f64(gate) * y
    return out

@@ -1,0 +1,184 @@
+from contextlib import ExitStack
+
+import concourse.mybir as mybir
+
+K, T, E, C, N = 2048, 512, 2, 256, 256
+P = 128
+PASSES = K // 512
+FLOPS = 2 * E * C * K * N
+
+F32 = mybir.dt.float32
+BF16 = mybir.dt.bfloat16
+I32 = mybir.dt.int32
+U32 = mybir.dt.uint32
+U16 = mybir.dt.uint16
+U8 = mybir.dt.uint8
+FP8X4 = mybir.dt.float8_e4m3fn_x4
+FP4X4 = mybir.dt.float4_e2m1fn_x4
+COPY = mybir.ActivationFunctionType.Copy
+MULT = mybir.AluOpType.mult
+ADD = mybir.AluOpType.add
+
+PLAN = {
+    (0, 0): ("VG", "V"),
+    (0, 1): ("SG", "V"),
+    (1, 0): ("G", "S"),
+    (1, 1): ("VG", "V"),
+    (2, 0): ("G", "V"),
+    (2, 1): ("G", "V"),
+    (3, 0): ("SG", "S"),
+    (3, 1): ("SG", "V"),
+}
+
+
+def tile_moe_two_lin_none_kernel(tc, xT, w_words, w_scales, gate, offs, dst, out):
+    nc = tc.nc
+    x_view = xT.rearrange("(a p j) t -> a p j t", p=P, j=4)
+    words_view = w_words.bitcast(I32)
+    scales_view = w_scales.bitcast(I32)
+
+    with ExitStack() as ctx:
+        keep = ctx.enter_context(tc.tile_pool(name="keep", bufs=1))
+        psum = ctx.enter_context(tc.psum_pool(name="psum", bufs=1))
+
+        offs_sb = keep.tile([P, T // 16], U16, name="offs_sb")
+        dst_sb = keep.tile([P, T // 16], U16, name="dst_sb")
+        scale_sb = keep.tile([P, E * PASSES, N], U8, name="scale_sb", align_bytes=64)
+        nc.vector.memset(scale_sb[:].rearrange("p g n -> p (g n)").bitcast(I32), 0)
+
+        raw = {}
+        words = {}
+
+        def load_x(a, u):
+            raw[a, u] = keep.tile([P, 2, T], F32, name="raw%d%d" % (a, u), align_bytes=64)
+            nc.sync.dma_start(raw[a, u][:], x_view[a, :, 2 * u : 2 * u + 2, :])
+
+        def load_words(a):
+            words[a] = keep.tile([P, E, 2 * N], U8, name="words%d" % a, align_bytes=64)
+            nc.sync.dma_start(words[a][:].bitcast(I32), words_view[:, a].rearrange("e p b -> p e b"))
+
+        for q in range(4):
+            nc.scalar.dma_start(
+                scale_sb[32 * q : 32 * q + 4].bitcast(I32),
+                scales_view[:, :, 4 * q : 4 * q + 4, :].rearrange("e a q n -> q (e a) n"),
+            )
+        load_x(0, 0)
+        nc.sync.dma_start(offs_sb[:], offs)
+        load_x(0, 1)
+        load_x(1, 0)
+        load_x(1, 1)
+        load_x(2, 0)
+        load_x(2, 1)
+        load_x(3, 0)
+        load_x(3, 1)
+        load_words(0)
+        load_words(1)
+        load_words(2)
+        load_words(3)
+        nc.sync.dma_start(dst_sb[:], dst)
+        gates = []
+        for h in range(2):
+            g = keep.tile([P, E * C], F32, name="gate%d" % h, align_bytes=64)
+            nc.sync.dma_start(g[:], gate[h * P : (h + 1) * P, :])
+            gates.append(g)
+
+        acc = {}
+        for e in range(E):
+            for h in range(2):
+                for s in range(2):
+                    acc[e, h, s] = psum.tile([P, 128], F32, name="acc%d%d%d" % (e, h, s))
+
+        def cast(engine, dest, src):
+            if engine == "V":
+                nc.vector.tensor_copy(out=dest, in_=src)
+            elif engine == "S":
+                nc.scalar.copy(out=dest, in_=src)
+            else:
+                nc.gpsimd.tensor_scalar(out=dest, in0=src, scalar1=1.0, scalar2=0.0, op0=MULT, op1=ADD)
+
+        grouped, codes, scales, rounded = {}, {}, {}, {}
+
+        def cast_unit(a, u):
+            casters, gatherer = PLAN[a, u]
+            if gatherer == "V":
+                rounded[a, u] = keep.tile([P, T, 2], BF16, name="pair%d%d" % (a, u), align_bytes=64)
+                width = T // len(casters)
+                for i, engine in enumerate(casters):
+                    cols = slice(i * width, (i + 1) * width)
+                    cast(engine, rounded[a, u][:, cols, :], raw[a, u][:, :, cols].rearrange("p j t -> p t j"))
+            else:
+                rounded[a, u] = keep.tile([P, 2, T], BF16, name="planes%d%d" % (a, u), align_bytes=64)
+                step = 2 // len(casters)
+                for i, engine in enumerate(casters):
+                    rows = slice(i * step, (i + 1) * step)
+                    cast(engine, rounded[a, u][:, rows, :], raw[a, u][:, rows, :])
+
+        def gather_unit(a, u, e):
+            flat = grouped[a][:].rearrange("p s j -> p (s j)")
+            slots = slice(e * C, (e + 1) * C)
+            columns = offs_sb[:, 16 * e : 16 * (e + 1)]
+            if PLAN[a, u][1] == "V":
+                window = rounded[a, u][:].rearrange("p t j -> p (t j)").bitcast(U32)
+                nc.vector.tensor_copy(
+                    out=flat.bitcast(U32).rearrange("p (s u) -> p s u", u=2)[:, slots, u],
+                    in_=window.indirect(columns),
+                )
+            else:
+                for j in range(2):
+                    nc.scalar.activation(grouped[a][:, slots, 2 * u + j], rounded[a, u][:, j, :].indirect(columns), COPY)
+
+        def quantize(a, s0, s1):
+            nc.vector.quantize_mx(
+                out=codes[a][:, s0:s1].bitcast(FP8X4),
+                scales=scales[a][:, s0:s1],
+                in_=grouped[a][:, s0:s1, :].rearrange("p s j -> p (s j)"),
+            )
+
+        def multiply(a, e):
+            for h in range(2):
+                for s in range(2):
+                    cols = slice(e * C + s * 128, e * C + (s + 1) * 128)
+                    nc.tensor.matmul_mx(
+                        out=acc[e, h, s][:],
+                        lhsT=words[a][:, e, h * 256 : (h + 1) * 256].bitcast(FP4X4),
+                        lhsT_scale=scale_sb[:, e * PASSES + a, h * 128 : (h + 1) * 128],
+                        rhs=codes[a][:, cols].bitcast(FP8X4),
+                        rhs_scale=scales[a][:, cols],
+                        start=(a == 0),
+                        stop=(a == PASSES - 1),
+                    )
+
+        for a in range(PASSES):
+            grouped[a] = keep.tile([P, E * C, 4], BF16, name="grouped%d" % a, align_bytes=64)
+            codes[a] = keep.tile([P, E * C], U32, name="codes%d" % a, align_bytes=64)
+            scales[a] = keep.tile([P, E * C], U8, name="scales%d" % a, align_bytes=64)
+            for u in range(2):
+                cast_unit(a, u)
+            if a < PASSES - 1:
+                for u in range(2):
+                    for e in range(E):
+                        gather_unit(a, u, e)
+                quantize(a, 0, E * C)
+                for e in range(E):
+                    multiply(a, e)
+            else:
+                for e in range(E):
+                    for u in range(2):
+                        gather_unit(a, u, e)
+                    quantize(a, e * C, (e + 1) * C)
+                    multiply(a, e)
+
+        placed = [keep.tile([P, T], F32, name="placed%d" % h, align_bytes=64) for h in range(2)]
+        for e in range(E):
+            for h in range(2):
+                y = keep.tile([P, C], F32, name="y%d%d" % (e, h), align_bytes=64)
+                for s in range(2):
+                    nc.scalar.copy(out=y[:, s * 128 : (s + 1) * 128], in_=acc[e, h, s][:])
+                nc.vector.tensor_tensor(
+                    out=placed[h][:].indirect(dst_sb[:, 16 * e : 16 * (e + 1)]),
+                    in0=y[:],
+                    in1=gates[h][:, e * C : (e + 1) * C],
+                    op=MULT,
+                )
+        for h in range(2):
+            nc.sync.dma_start(out[h * P : (h + 1) * P, :], placed[h][:])

@@ -5,6 +5,7 @@ import concourse.mybir as mybir
 K, T, E, C, N = 2048, 512, 2, 256, 256
 P = 128
 PASSES = K // 512
+WIDE = 704
 FLOPS = 2 * E * C * K * N
 
 F32 = mybir.dt.float32
@@ -15,25 +16,21 @@ U16 = mybir.dt.uint16
 U8 = mybir.dt.uint8
 FP8X4 = mybir.dt.float8_e4m3fn_x4
 FP4X4 = mybir.dt.float4_e2m1fn_x4
-COPY = mybir.ActivationFunctionType.Copy
 MULT = mybir.AluOpType.mult
-ADD = mybir.AluOpType.add
 
-PLAN = {
-    (0, 0): ("VG", "V"),
-    (0, 1): ("SG", "V"),
-    (1, 0): ("G", "S"),
-    (1, 1): ("VG", "V"),
-    (2, 0): ("G", "V"),
-    (2, 1): ("G", "V"),
-    (3, 0): ("SG", "S"),
-    (3, 1): ("SG", "V"),
-}
+LOADS = (((0, 512),), ((0, 512),), ((0, 512),), ((0, 512),))
+CASTS = (
+    (("S", 0, 208), ("V", 208, 512),),
+    (("S", 0, 352), ("V", 352, 512),),
+    (("S", 0, 400), ("V", 400, 512),),
+    (("S", 0, 512),),
+)
+QUANTS = (((0, 512),), ((0, 512),), ((0, 512),), ((0, 512),))
 
 
 def tile_moe_two_lin_none_kernel(tc, xT, w_words, w_scales, gate, offs, dst, out):
     nc = tc.nc
-    x_view = xT.rearrange("(a p j) t -> a p j t", p=P, j=4)
+    x_view = xT.rearrange("(a p j) t -> p a j t", p=P, j=4)
     words_view = w_words.bitcast(I32)
     scales_view = w_scales.bitcast(I32)
 
@@ -45,36 +42,27 @@ def tile_moe_two_lin_none_kernel(tc, xT, w_words, w_scales, gate, offs, dst, out
         dst_sb = keep.tile([P, T // 16], U16, name="dst_sb")
         scale_sb = keep.tile([P, E * PASSES, N], U8, name="scale_sb", align_bytes=64)
         nc.vector.memset(scale_sb[:].rearrange("p g n -> p (g n)").bitcast(I32), 0)
-
-        raw = {}
-        words = {}
-
-        def load_x(a, u):
-            raw[a, u] = keep.tile([P, 2, T], F32, name="raw%d%d" % (a, u), align_bytes=64)
-            nc.sync.dma_start(raw[a, u][:], x_view[a, :, 2 * u : 2 * u + 2, :])
-
-        def load_words(a):
-            words[a] = keep.tile([P, E, 2 * N], U8, name="words%d" % a, align_bytes=64)
-            nc.sync.dma_start(words[a][:].bitcast(I32), words_view[:, a].rearrange("e p b -> p e b"))
-
+        zeroed = {}
+        for name in ("pack", "last", "moved1", "moved2"):
+            zeroed[name] = keep.tile([P, WIDE if name == "pack" else T], U8, name=name, align_bytes=64)
+            nc.vector.memset(zeroed[name][:].bitcast(I32), 0)
+        pack, last = zeroed["pack"], zeroed["last"]
         for q in range(4):
             nc.scalar.dma_start(
                 scale_sb[32 * q : 32 * q + 4].bitcast(I32),
                 scales_view[:, :, 4 * q : 4 * q + 4, :].rearrange("e a q n -> q (e a) n"),
             )
-        load_x(0, 0)
-        nc.sync.dma_start(offs_sb[:], offs)
-        load_x(0, 1)
-        load_x(1, 0)
-        load_x(1, 1)
-        load_x(2, 0)
-        load_x(2, 1)
-        load_x(3, 0)
-        load_x(3, 1)
-        load_words(0)
-        load_words(1)
-        load_words(2)
-        load_words(3)
+
+        raw, words = {}, {}
+        for a in range(PASSES):
+            for c0, c1 in LOADS[a]:
+                raw[a, c0] = keep.tile([P, 4, c1 - c0], F32, name="raw%d_%d" % (a, c0), align_bytes=64)
+                nc.sync.dma_start(raw[a, c0][:], x_view[:, a, :, c0:c1])
+                if a == 0 and c0 == 0:
+                    nc.sync.dma_start(offs_sb[:], offs)
+        for a in range(PASSES):
+            words[a] = keep.tile([P, E, 2 * N], U8, name="words%d" % a, align_bytes=64)
+            nc.sync.dma_start(words[a][:].bitcast(I32), words_view[:, a].rearrange("e p b -> p e b"))
         nc.sync.dma_start(dst_sb[:], dst)
         gates = []
         for h in range(2):
@@ -88,51 +76,26 @@ def tile_moe_two_lin_none_kernel(tc, xT, w_words, w_scales, gate, offs, dst, out
                 for s in range(2):
                     acc[e, h, s] = psum.tile([P, 128], F32, name="acc%d%d%d" % (e, h, s))
 
-        def cast(engine, dest, src):
+        rounded, codes, slot_codes = {}, {}, {}
+
+        def cast(a, engine, c0, c1):
+            base = max(lo for lo, hi in LOADS[a] if lo <= c0)
+            dest = rounded[a][:, c0:c1, :].rearrange("p (c i) j -> p c j i", i=4)
+            src = raw[a, base][:, :, c0 - base : c1 - base].rearrange("p j (c i) -> p c j i", i=4)
             if engine == "V":
                 nc.vector.tensor_copy(out=dest, in_=src)
-            elif engine == "S":
+            else:
                 nc.scalar.copy(out=dest, in_=src)
-            else:
-                nc.gpsimd.tensor_scalar(out=dest, in0=src, scalar1=1.0, scalar2=0.0, op0=MULT, op1=ADD)
 
-        grouped, codes, scales, rounded = {}, {}, {}, {}
+        slot_pack = keep.tile([P, E * C], U8, name="slot_pack", align_bytes=64)
+        slot_last = keep.tile([P, E * C], U8, name="slot_last", align_bytes=64)
+        slot_scales = {0: slot_pack, 1: zeroed["moved1"], 2: zeroed["moved2"], 3: slot_last}
 
-        def cast_unit(a, u):
-            casters, gatherer = PLAN[a, u]
-            if gatherer == "V":
-                rounded[a, u] = keep.tile([P, T, 2], BF16, name="pair%d%d" % (a, u), align_bytes=64)
-                width = T // len(casters)
-                for i, engine in enumerate(casters):
-                    cols = slice(i * width, (i + 1) * width)
-                    cast(engine, rounded[a, u][:, cols, :], raw[a, u][:, :, cols].rearrange("p j t -> p t j"))
-            else:
-                rounded[a, u] = keep.tile([P, 2, T], BF16, name="planes%d%d" % (a, u), align_bytes=64)
-                step = 2 // len(casters)
-                for i, engine in enumerate(casters):
-                    rows = slice(i * step, (i + 1) * step)
-                    cast(engine, rounded[a, u][:, rows, :], raw[a, u][:, rows, :])
+        def gather(dest, window, e):
+            nc.vector.tensor_copy(out=dest[:, e * C : (e + 1) * C], in_=window[:].indirect(offs_sb[:, 16 * e : 16 * (e + 1)]))
 
-        def gather_unit(a, u, e):
-            flat = grouped[a][:].rearrange("p s j -> p (s j)")
-            slots = slice(e * C, (e + 1) * C)
-            columns = offs_sb[:, 16 * e : 16 * (e + 1)]
-            if PLAN[a, u][1] == "V":
-                window = rounded[a, u][:].rearrange("p t j -> p (t j)").bitcast(U32)
-                nc.vector.tensor_copy(
-                    out=flat.bitcast(U32).rearrange("p (s u) -> p s u", u=2)[:, slots, u],
-                    in_=window.indirect(columns),
-                )
-            else:
-                for j in range(2):
-                    nc.scalar.activation(grouped[a][:, slots, 2 * u + j], rounded[a, u][:, j, :].indirect(columns), COPY)
-
-        def quantize(a, s0, s1):
-            nc.vector.quantize_mx(
-                out=codes[a][:, s0:s1].bitcast(FP8X4),
-                scales=scales[a][:, s0:s1],
-                in_=grouped[a][:, s0:s1, :].rearrange("p s j -> p (s j)"),
-            )
+        def gather_all(dest, window):
+            nc.vector.tensor_copy(out=dest[:], in_=window[:].indirect(offs_sb[:]))
 
         def multiply(a, e):
             for h in range(2):
@@ -142,31 +105,47 @@ def tile_moe_two_lin_none_kernel(tc, xT, w_words, w_scales, gate, offs, dst, out
                         out=acc[e, h, s][:],
                         lhsT=words[a][:, e, h * 256 : (h + 1) * 256].bitcast(FP4X4),
                         lhsT_scale=scale_sb[:, e * PASSES + a, h * 128 : (h + 1) * 128],
-                        rhs=codes[a][:, cols].bitcast(FP8X4),
-                        rhs_scale=scales[a][:, cols],
+                        rhs=slot_codes[a][:, cols].bitcast(FP8X4),
+                        rhs_scale=slot_scales[a][:, cols],
                         start=(a == 0),
                         stop=(a == PASSES - 1),
                     )
 
         for a in range(PASSES):
-            grouped[a] = keep.tile([P, E * C, 4], BF16, name="grouped%d" % a, align_bytes=64)
-            codes[a] = keep.tile([P, E * C], U32, name="codes%d" % a, align_bytes=64)
-            scales[a] = keep.tile([P, E * C], U8, name="scales%d" % a, align_bytes=64)
-            for u in range(2):
-                cast_unit(a, u)
-            if a < PASSES - 1:
-                for u in range(2):
-                    for e in range(E):
-                        gather_unit(a, u, e)
-                quantize(a, 0, E * C)
-                for e in range(E):
-                    multiply(a, e)
+            rounded[a] = keep.tile([P, T, 4], BF16, name="rounded%d" % a, align_bytes=64)
+            codes[a] = keep.tile([P, T if a == 3 else WIDE], U32, name="codes%d" % a, align_bytes=64)
+            if a < 3:
+                nc.vector.memset(codes[a][:, T:WIDE].bitcast(I32), 0)
+            slot_codes[a] = keep.tile([P, E * C], U32, name="slot_codes%d" % a, align_bytes=64)
+            for engine, c0, c1 in CASTS[a]:
+                cast(a, engine, c0, c1)
+            for c0, c1 in QUANTS[a]:
+                nc.vector.quantize_mx(
+                    out=codes[a][:, c0:c1].bitcast(FP8X4),
+                    scales=last[:, c0:c1] if a == 3 else pack[4 * a : P, c0:c1],
+                    in_=rounded[a][:, c0:c1, :].rearrange("p t j -> p (t j)"),
+                )
+            if a == 2:
+                gather_all(slot_pack, pack)
+                for b in (1, 2):
+                    for q in range(4):
+                        nc.sync.dma_start(
+                            slot_scales[b][32 * q : 32 * q + 4, :].bitcast(I32),
+                            slot_pack[32 * q + 4 * b : 32 * q + 4 * b + 4, :].bitcast(I32),
+                        )
+            if a < 3:
+                gather_all(slot_codes[a], codes[a])
             else:
                 for e in range(E):
-                    for u in range(2):
-                        gather_unit(a, u, e)
-                    quantize(a, e * C, (e + 1) * C)
+                    gather(slot_last, last, e)
+                    gather(slot_codes[a], codes[a], e)
                     multiply(a, e)
+            if a == 2:
+                for e in range(E):
+                    multiply(0, e)
+                for e in range(E):
+                    multiply(1, e)
+                    multiply(2, e)
 
         placed = [keep.tile([P, T], F32, name="placed%d" % h, align_bytes=64) for h in range(2)]
         for e in range(E):

from contextlib import ExitStack

import concourse.mybir as mybir

K, T, E, C, N = 2048, 512, 2, 256, 256
P = 128
PASSES = K // 512
WIDE = 704
FLOPS = 2 * E * C * K * N

F32 = mybir.dt.float32
BF16 = mybir.dt.bfloat16
I32 = mybir.dt.int32
U32 = mybir.dt.uint32
U16 = mybir.dt.uint16
U8 = mybir.dt.uint8
FP8X4 = mybir.dt.float8_e4m3fn_x4
FP4X4 = mybir.dt.float4_e2m1fn_x4
MULT = mybir.AluOpType.mult

LOADS = (((0, 512),), ((0, 512),), ((0, 512),), ((0, 512),))
CASTS = (
    (("S", 0, 208), ("V", 208, 512),),
    (("S", 0, 352), ("V", 352, 512),),
    (("S", 0, 400), ("V", 400, 512),),
    (("S", 0, 512),),
)
QUANTS = (((0, 512),), ((0, 512),), ((0, 512),), ((0, 512),))


def tile_moe_two_lin_none_kernel(tc, xT, w_words, w_scales, gate, offs, dst, out):
    nc = tc.nc
    x_view = xT.rearrange("(a p j) t -> p a j t", p=P, j=4)
    words_view = w_words.bitcast(I32)
    scales_view = w_scales.bitcast(I32)

    with ExitStack() as ctx:
        keep = ctx.enter_context(tc.tile_pool(name="keep", bufs=1))
        psum = ctx.enter_context(tc.psum_pool(name="psum", bufs=1))

        offs_sb = keep.tile([P, T // 16], U16, name="offs_sb")
        dst_sb = keep.tile([P, T // 16], U16, name="dst_sb")
        scale_sb = keep.tile([P, E * PASSES, N], U8, name="scale_sb", align_bytes=64)
        nc.vector.memset(scale_sb[:].rearrange("p g n -> p (g n)").bitcast(I32), 0)
        zeroed = {}
        for name in ("pack", "last", "moved1", "moved2"):
            zeroed[name] = keep.tile([P, WIDE if name == "pack" else T], U8, name=name, align_bytes=64)
            nc.vector.memset(zeroed[name][:].bitcast(I32), 0)
        pack, last = zeroed["pack"], zeroed["last"]
        for q in range(4):
            nc.scalar.dma_start(
                scale_sb[32 * q : 32 * q + 4].bitcast(I32),
                scales_view[:, :, 4 * q : 4 * q + 4, :].rearrange("e a q n -> q (e a) n"),
            )

        raw, words = {}, {}
        for a in range(PASSES):
            for c0, c1 in LOADS[a]:
                raw[a, c0] = keep.tile([P, 4, c1 - c0], F32, name="raw%d_%d" % (a, c0), align_bytes=64)
                nc.sync.dma_start(raw[a, c0][:], x_view[:, a, :, c0:c1])
                if a == 0 and c0 == 0:
                    nc.sync.dma_start(offs_sb[:], offs)
        for a in range(PASSES):
            words[a] = keep.tile([P, E, 2 * N], U8, name="words%d" % a, align_bytes=64)
            nc.sync.dma_start(words[a][:].bitcast(I32), words_view[:, a].rearrange("e p b -> p e b"))
        nc.sync.dma_start(dst_sb[:], dst)
        gates = []
        for h in range(2):
            g = keep.tile([P, E * C], F32, name="gate%d" % h, align_bytes=64)
            nc.sync.dma_start(g[:], gate[h * P : (h + 1) * P, :])
            gates.append(g)

        acc = {}
        for e in range(E):
            for h in range(2):
                for s in range(2):
                    acc[e, h, s] = psum.tile([P, 128], F32, name="acc%d%d%d" % (e, h, s))

        rounded, codes, slot_codes = {}, {}, {}

        def cast(a, engine, c0, c1):
            base = max(lo for lo, hi in LOADS[a] if lo <= c0)
            dest = rounded[a][:, c0:c1, :].rearrange("p (c i) j -> p c j i", i=4)
            src = raw[a, base][:, :, c0 - base : c1 - base].rearrange("p j (c i) -> p c j i", i=4)
            if engine == "V":
                nc.vector.tensor_copy(out=dest, in_=src)
            else:
                nc.scalar.copy(out=dest, in_=src)

        slot_pack = keep.tile([P, E * C], U8, name="slot_pack", align_bytes=64)
        slot_last = keep.tile([P, E * C], U8, name="slot_last", align_bytes=64)
        slot_scales = {0: slot_pack, 1: zeroed["moved1"], 2: zeroed["moved2"], 3: slot_last}

        def gather(dest, window, e):
            nc.vector.tensor_copy(out=dest[:, e * C : (e + 1) * C], in_=window[:].indirect(offs_sb[:, 16 * e : 16 * (e + 1)]))

        def gather_all(dest, window):
            nc.vector.tensor_copy(out=dest[:], in_=window[:].indirect(offs_sb[:]))

        def multiply(a, e):
            for h in range(2):
                for s in range(2):
                    cols = slice(e * C + s * 128, e * C + (s + 1) * 128)
                    nc.tensor.matmul_mx(
                        out=acc[e, h, s][:],
                        lhsT=words[a][:, e, h * 256 : (h + 1) * 256].bitcast(FP4X4),
                        lhsT_scale=scale_sb[:, e * PASSES + a, h * 128 : (h + 1) * 128],
                        rhs=slot_codes[a][:, cols].bitcast(FP8X4),
                        rhs_scale=slot_scales[a][:, cols],
                        start=(a == 0),
                        stop=(a == PASSES - 1),
                    )

        for a in range(PASSES):
            rounded[a] = keep.tile([P, T, 4], BF16, name="rounded%d" % a, align_bytes=64)
            codes[a] = keep.tile([P, T if a == 3 else WIDE], U32, name="codes%d" % a, align_bytes=64)
            if a < 3:
                nc.vector.memset(codes[a][:, T:WIDE].bitcast(I32), 0)
            slot_codes[a] = keep.tile([P, E * C], U32, name="slot_codes%d" % a, align_bytes=64)
            for engine, c0, c1 in CASTS[a]:
                cast(a, engine, c0, c1)
            for c0, c1 in QUANTS[a]:
                nc.vector.quantize_mx(
                    out=codes[a][:, c0:c1].bitcast(FP8X4),
                    scales=last[:, c0:c1] if a == 3 else pack[4 * a : P, c0:c1],
                    in_=rounded[a][:, c0:c1, :].rearrange("p t j -> p (t j)"),
                )
            if a == 2:
                gather_all(slot_pack, pack)
                for b in (1, 2):
                    for q in range(4):
                        nc.sync.dma_start(
                            slot_scales[b][32 * q : 32 * q + 4, :].bitcast(I32),
                            slot_pack[32 * q + 4 * b : 32 * q + 4 * b + 4, :].bitcast(I32),
                        )
            if a < 3:
                gather_all(slot_codes[a], codes[a])
            else:
                for e in range(E):
                    gather(slot_last, last, e)
                    gather(slot_codes[a], codes[a], e)
                    multiply(a, e)
            if a == 2:
                for e in range(E):
                    multiply(0, e)
                for e in range(E):
                    multiply(1, e)
                    multiply(2, e)

        placed = [keep.tile([P, T], F32, name="placed%d" % h, align_bytes=64) for h in range(2)]
        for e in range(E):
            for h in range(2):
                y = keep.tile([P, C], F32, name="y%d%d" % (e, h), align_bytes=64)
                for s in range(2):
                    nc.scalar.copy(out=y[:, s * 128 : (s + 1) * 128], in_=acc[e, h, s][:])
                nc.vector.tensor_tensor(
                    out=placed[h][:].indirect(dst_sb[:, 16 * e : 16 * (e + 1)]),
                    in0=y[:],
                    in1=gates[h][:, e * C : (e + 1) * C],
                    op=MULT,
                )
        for h in range(2):
            nc.sync.dma_start(out[h * P : (h + 1) * P, :], placed[h][:])
